import numpy as np
import ml_dtypes


def mxq(x, axis, fmt="e4m3"):
    dtype, down = {"e4m3": (ml_dtypes.float8_e4m3fn, 7), "e5m2": (ml_dtypes.float8_e5m2, 14)}[fmt]
    v = np.moveaxis(np.asarray(x, np.float32).astype(ml_dtypes.bfloat16).astype(np.float64), axis, -1)
    blocks = v.reshape(v.shape[:-1] + (-1, 32))
    amax = np.abs(blocks).max(-1, keepdims=True)
    byte = np.maximum(np.where(amax > 0, np.frexp(amax)[1] - 1 + 127, 0) - down, 1)
    scale = np.exp2(byte - 127.0)
    codes = (blocks / scale).astype(np.float32).astype(dtype).astype(np.float64)
    return np.moveaxis((codes * scale).reshape(v.shape), -1, axis)


WIDE = False


def mx_kscale(k):
    if not WIDE:
        return np.ones(k)
    levels = np.array([10, -10, 5, -5, 0])
    if k % 512:
        return np.exp2(np.random.permutation(np.resize(levels, k // 32))).repeat(32)
    a = np.empty((k // 512, 16))
    for p in range(k // 512):
        a[p, :8] = np.random.permutation(np.resize(levels, 8))
        for g in range(8):
            far = levels[np.abs(levels - a[p, g]) >= 10]
            a[p, g + 8] = far[np.random.randint(len(far))]
    return np.exp2(a.ravel()).repeat(32)


def f64(x):
    return np.asarray(x).astype(np.float64)


def striped(idx):
    return np.tile(idx.reshape(-1, 16).T, (8, 1)).astype(np.uint16)


def unstriped(offs):
    return offs[:16].T.reshape(-1).astype(np.int64)


E2M1 = np.array([0.0, 0.5, 1.0, 1.5, 2.0, 3.0, 4.0, 6.0, -0.0, -0.5, -1.0, -1.5, -2.0, -3.0, -4.0, -6.0])


def pack_weight(w, fmt):
    k, n = w.shape
    w = f64(np.asarray(w, np.float32).astype(ml_dtypes.bfloat16)).reshape(k // 32, 32, n)
    amax = np.abs(w).max(1)
    if fmt == "e4m3":
        byte = np.frexp(amax)[1] - 1 + 127 - 7
    else:
        mant, ex = np.frexp(amax / 6.0)
        byte = np.where(mant > 0.5, ex, ex - 1) + 127
    byte = np.clip(np.where(amax > 0, byte, 1), 1, 254)
    scaled = (w * np.exp2(127.0 - byte)[:, None, :]).reshape(k, n).astype(np.float32)
    by_word = np.ascontiguousarray(scaled.reshape(k // 512, 128, 4, n).transpose(0, 1, 3, 2))
    if fmt == "e4m3":
        words = by_word.astype(ml_dtypes.float8_e4m3fn).view(np.uint8)
    else:
        c = by_word.astype(ml_dtypes.float4_e2m1fn).view(np.uint8) & 0xF
        words = (c[..., 0::2] | (c[..., 1::2] << 4)).reshape(k // 512, 128, 2 * n)
    return np.ascontiguousarray(words), np.ascontiguousarray(byte.astype(np.uint8).reshape(k // 512, 16, n))


def unpack_weight(words, scales, fmt):
    g, _, n = scales.shape
    words = np.ascontiguousarray(words).reshape(g, 128, n, -1)
    if fmt == "e4m3":
        vals = words.view(ml_dtypes.float8_e4m3fn).astype(np.float64)
    else:
        nib = np.empty((g, 128, n, 4), np.uint8)
        nib[..., 0::2] = words & 0xF
        nib[..., 1::2] = words >> 4
        vals = E2M1[nib]
    vals = vals * np.repeat(np.exp2(scales.astype(np.float64) - 127.0), 8, axis=1)[..., None]
    return vals.transpose(0, 1, 3, 2).reshape(g * 512, n)


def gelu(v):
    return 0.5 * v * (1.0 + np.tanh(np.sqrt(2.0 / np.pi) * (v + 0.044715 * v**3)))


K, H, T, S, T2, P, B = 1024, 1024, 2048, 512, 1024, 512, 128

def setup_inputs():
    n = np.random.standard_normal
    s = mx_kscale(K)[:, None]
    u = mx_kscale(H)[:, None]
    d = {}
    d["tab_words"], d["tab_scales"] = pack_weight(n((K, T)) * s, "e4m3")
    d["offs"] = striped(np.random.permutation(T)[:S])
    d["w1"] = (n((K, H)) / s * u.T / K ** 0.5).astype(np.float32)
    d["cap"] = ((0.3 + 0.5 * n(H)) * u[:, 0]).astype(np.float32)
    d["season"] = (0.7 * n((H, S)) * u).astype(np.float32)
    d["low"] = ((0.5 * n(H) - 0.5) * u[:, 0]).astype(np.float32)
    d["wgs"] = np.exp(0.3 * n((B, S))).astype(np.float32)
    d["page0"] = (n((H, T2)) * u).astype(np.float32)
    d["offs2"] = striped(np.random.permutation(T2)[:S])
    d["offs3"] = striped(np.random.permutation(T2)[:P])
    d["w4_words"], d["w4_scales"] = pack_weight(n((H, H)) / u * u.T / H ** 0.5, "e2m1")
    d["gain"] = (n(H) / u[:, 0] ** 2 / H ** 0.5).astype(np.float32)
    d["base"] = (0.8 * n((T2, P))).astype(np.float32)
    d["slot"] = np.exp(0.4 * n(T2)).astype(np.float32)
    return d

def reference(tab_words, tab_scales, offs, w1, cap, season, low, wgs, page0, offs2, offs3, w4_words, w4_scales, gain, base, slot):
    v = unpack_weight(tab_words, tab_scales, "e4m3")[:, unstriped(offs)]
    b = mxq(f64(w1), 0, "e4m3").T @ v
    h = np.maximum(np.minimum(b, f64(cap)[:, None]) + f64(season), f64(low)[:, None])
    page = f64(page0).copy()
    page[:, unstriped(offs2)] = np.tile(f64(wgs), (H // B, 1)) * h
    x0 = page[:, unstriped(offs3)]
    w4 = unpack_weight(w4_words, w4_scales, "e2m1")
    y = w4.T @ mxq(x0, 0, "e4m3")
    x = np.minimum(x0, y) * f64(gain)[:, None]
    e = mxq(page, 0, "e4m3").T @ mxq(x, 0, "e4m3")
    return (e - f64(base)) * f64(slot)[:, None]

@@ -1,0 +1,343 @@
+from contextlib import ExitStack
+
+import concourse.mybir as mybir
+
+K, H, T, S, T2, NP = 1024, 1024, 2048, 512, 1024, 512
+FLOPS = 2 * K * H * S + 2 * H * H * NP + 2 * H * T2 * NP
+
+F32 = mybir.dt.float32
+BF16 = mybir.dt.bfloat16
+I32 = mybir.dt.int32
+U32 = mybir.dt.uint32
+U16 = mybir.dt.uint16
+U8 = mybir.dt.uint8
+FP8X4 = mybir.dt.float8_e4m3fn_x4
+FP4X4 = mybir.dt.float4_e2m1fn_x4
+ALU = mybir.AluOpType
+ACT = mybir.ActivationFunctionType
+
+P = 128
+PACK = 4
+KP = 512
+PASSES = 2
+SLICES = 8
+V_SHARE_W1 = 84
+V_SHARE_X0 = 340
+
+
+def tile_list_salt_pond_readout_kernel(
+    tc, tab_words, tab_scales, offs, w1, cap, season, low, wgs, page0, offs2, offs3,
+    w4_words, w4_scales, gain, base, slot, out,
+):
+    nc = tc.nc
+    with ExitStack() as ctx:
+        keep = ctx.enter_context(tc.tile_pool(name="keep", bufs=1))
+        ring = ctx.enter_context(tc.tile_pool(name="ring", bufs=1))
+        psum = ctx.enter_context(tc.psum_pool(name="psum", bufs=1))
+
+        def kept(shape, dtype, name):
+            return keep.tile(shape, dtype, name=name, align_bytes=64)
+
+        def shared(tag, shape, dtype, name):
+            return ring.tile(shape, dtype, name=name, tag=tag, bufs=1, align_bytes=64)
+
+        def big(name):
+            return ring.tile([P, PACK, KP], F32, name=name, tag="big", bufs=4, align_bytes=64)
+
+        def grouped(name):
+            return ring.tile([P, KP * PACK], BF16, name=name, tag="grouped", bufs=4, align_bytes=64)
+
+        def bank(i, name):
+            return psum.tile([P, KP], F32, name=name, tag="bank%d" % i)
+
+        list1 = kept([P, S // 16], U16, "list1")
+        list2 = kept([P, S // 16], U16, "list2")
+        list3 = kept([P, NP // 16], U16, "list3")
+
+        tab_sc = kept([P, T], U8, "tab_sc")
+        w4_sc_raw = kept([P, PASSES, H], U8, "w4_sc_raw")
+        nc.vector.memset(w4_sc_raw[:].rearrange("p a n -> p (a n)").bitcast(I32), 0)
+        nc.vector.memset(tab_sc[:].bitcast(I32), 0)
+
+        w4_raw = kept([P, PASSES, 2 * H], U8, "w4_raw")
+        nc.sync.dma_start(out=w4_raw[:].bitcast(I32), in_=w4_words.rearrange("a p n -> p a n").bitcast(I32))
+        tab_w = [shared("tab%d" % a, [P, T], I32, "tab_w%d" % a) for a in range(PASSES)]
+        w1_raw = {}
+
+        def load_tab(a):
+            nc.sync.dma_start(out=tab_w[a][:], in_=tab_words[a].rearrange("p t i -> p (t i)").bitcast(I32))
+
+        def load_w1(a, b):
+            w1_raw[a, b] = big("w1_raw%d%d" % (a, b))
+            nc.sync.dma_start(
+                out=w1_raw[a, b][:],
+                in_=w1[KP * a : KP * (a + 1), KP * b : KP * (b + 1)].rearrange("(p j) c -> p j c", j=PACK),
+            )
+
+        for q in range(4):
+            nc.sync.dma_start(
+                out=w4_sc_raw[32 * q : 32 * q + 4, :, :].bitcast(I32),
+                in_=w4_scales[:, 4 * q : 4 * q + 4, :].rearrange("a r n -> r a n").bitcast(I32),
+            )
+        load_w1(0, 0)
+        nc.sync.dma_start(list1[:], offs)
+        load_w1(1, 0)
+        for q in range(4):
+            nc.sync.dma_start(
+                out=tab_sc[32 * q : 32 * q + 8, :].bitcast(I32),
+                in_=tab_scales[:, 4 * q : 4 * q + 4, :].bitcast(I32),
+            )
+        cap_sb = kept([P, PASSES, PACK], F32, "cap_sb")
+        low_sb = kept([P, PASSES, PACK], F32, "low_sb")
+        gain_sb = kept([P, PASSES, PACK], F32, "gain_sb")
+        slot_sb = kept([P, SLICES], F32, "slot_sb")
+        load_tab(0)
+        load_tab(1)
+        nc.gpsimd.dma_start(out=cap_sb[:], in_=cap.rearrange("(b p t) -> p b t", b=PASSES, t=PACK))
+        nc.gpsimd.dma_start(out=low_sb[:], in_=low.rearrange("(b p t) -> p b t", b=PASSES, t=PACK))
+
+        w4_c = kept([P, PASSES * 2 * H], U8, "w4_c")
+        w4_s = kept([P, PASSES * H], U8, "w4_s")
+        nc.vector.tensor_copy(
+            out=w4_c[:].bitcast(U16).rearrange("p (g t q) -> p g q t", t=PACK, q=P),
+            in_=w4_raw[:].rearrange("p a n -> p (a n)").bitcast(U16).rearrange("p (g q t) -> p g q t", t=PACK, q=P),
+        )
+
+        nc.vector.tensor_copy(
+            out=w4_s[:].rearrange("p (g t q) -> p g q t", t=PACK, q=P),
+            in_=w4_sc_raw[:].rearrange("p a n -> p (a n)").rearrange("p (g q t) -> p g q t", t=PACK, q=P),
+        )
+
+        v_s = kept([P, S], U8, "v_s")
+        v_c = [kept([P, S], U32, "v_c%d" % a) for a in range(PASSES)]
+        nc.vector.tensor_copy(v_s[:], tab_sc[:].indirect(list1[:]))
+        nc.vector.tensor_copy(v_c[0][:], tab_w[0][:].bitcast(U32).indirect(list1[:]))
+        nc.vector.tensor_copy(v_c[1][:], tab_w[1][:].bitcast(U32).indirect(list1[:]))
+
+        season_rows = season.rearrange("(b p t) j -> b t p j", b=PASSES, t=PACK)
+        page_rows = page0.rearrange("(b p t) m -> b t p m", b=PASSES, t=PACK)
+        season_sb = [kept([P, S], F32, "season%d" % s) for s in range(SLICES)]
+        page = [kept([P, T2], F32, "page%d" % s) for s in range(SLICES)]
+        wgs_first = kept([P, 1, S], F32, "wgs_first")
+        wgs_rest = kept([P, PACK - 1, S], F32, "wgs_rest")
+        wgs_rows = wgs.rearrange("(p t) j -> p t j", t=PACK)
+        wgs_sb = [wgs_first[:, 0, :]] + [wgs_rest[:, t, :] for t in range(PACK - 1)]
+
+        def load_season(s):
+            nc.sync.dma_start(out=season_sb[s][:], in_=season_rows[s // PACK, s % PACK])
+
+        def load_page(s):
+            nc.sync.dma_start(out=page[s][:], in_=page_rows[s // PACK, s % PACK])
+
+        base_sb = []
+
+        def load_base(half):
+            tile = shared("tab%d" % half, [P, PACK, NP], F32, "base%d" % half)
+            base_sb.append(tile)
+            nc.sync.dma_start(
+                out=tile[:], in_=base[KP * half : KP * (half + 1), :].rearrange("(i p) j -> p i j", p=P)
+            )
+
+        nc.sync.dma_start(list2[:], offs2)
+        load_season(0)
+        for q in range(4):
+            nc.sync.dma_start(out=wgs_first[32 * q : 32 * q + 32, :, :], in_=wgs_rows[:, 0:1, :])
+        load_page(0)
+        load_season(1)
+        nc.sync.dma_start(list3[:], offs3)
+        for q in range(4):
+            nc.sync.dma_start(out=wgs_rest[32 * q : 32 * q + 32, :, :], in_=wgs_rows[:, 1:PACK, :])
+        load_page(1)
+        load_w1(0, 1)
+        load_season(2)
+        load_w1(1, 1)
+        load_season(3)
+        load_page(2)
+        nc.sync.dma_start(out=gain_sb[:], in_=gain.rearrange("(b p t) -> p b t", b=PASSES, t=PACK))
+        with nc.allow_non_contiguous_dma(reason="one value of slot for each output row"):
+            nc.sync.dma_start(out=slot_sb[:], in_=slot.rearrange("(i p) -> p i", p=P))
+        for s in range(3, SLICES):
+            if s + 1 < SLICES:
+                load_season(s + 1)
+            load_page(s)
+            if s in (4, 5):
+                load_base(s - 4)
+
+        def quantize(codes, scales, src):
+            nc.vector.quantize_mx(out=codes.bitcast(FP8X4), scales=scales, in_=src)
+
+        w1_c, w1_s = {}, {}
+
+        def prepare_w1(a, b, v_share):
+            g = grouped("w1_g%d%d" % (a, b))
+            dst = g[:].rearrange("p (t m j) -> p m j t", t=PACK, j=PACK)
+            src = w1_raw[a, b][:].rearrange("p j (m t) -> p m j t", t=PACK)
+            if v_share:
+                nc.vector.tensor_copy(out=dst[:, :v_share], in_=src[:, :v_share])
+            nc.scalar.copy(out=dst[:, v_share:], in_=src[:, v_share:])
+            w1_c[a, b] = shared("h%d" % (a + 1) if b else "w1_c%d" % a, [P, KP], U32, "w1_c%d%d" % (a, b))
+            w1_s[a, b] = kept([P, KP], U8, "w1_s%d%d" % (a, b))
+            quantize(w1_c[a, b][:], w1_s[a, b][:], g[:])
+
+        prepare_w1(0, 0, 0)
+        prepare_w1(1, 0, 0)
+
+        x0 = [kept([P, PACK, NP], F32, "x0_%d" % b) for b in range(PASSES)]
+        pairs = [kept([P, 2, T2, 2], BF16, "pairs%d" % b) for b in range(PASSES)]
+        x0_c, page_c = {}, {}
+        x0_s = [kept([P, NP], U8, "x0_s%d" % b) for b in range(PASSES)]
+        page_s = [kept([P, T2], U8, "page_s%d" % b) for b in range(PASSES)]
+        h = {}
+
+        def first_product(s):
+            b, t = divmod(s, PACK)
+            acc = bank(s, "h_acc%d" % s)
+            cols = slice(P * t, P * (t + 1))
+            for a in range(PASSES):
+                nc.tensor.matmul_mx(
+                    out=acc[:], lhsT=w1_c[a, b][:, cols].bitcast(FP8X4), lhsT_scale=w1_s[a, b][:, cols],
+                    rhs=v_c[a][:].bitcast(FP8X4), rhs_scale=v_s[4 * a : P, :],
+                    start=(a == 0), stop=(a == PASSES - 1),
+                )
+            h[s] = shared("h%d" % s, [P, S], F32, "h%d" % s)
+            nc.vector.scalar_tensor_tensor(
+                out=h[s][:], in0=acc[:], scalar=cap_sb[:, b, t : t + 1], in1=season_sb[s][:],
+                op0=ALU.min, op1=ALU.add,
+            )
+
+        def floor_h(s):
+            b, t = divmod(s, PACK)
+            nc.vector.tensor_scalar(out=h[s][:], in0=h[s][:], scalar1=low_sb[:, b, t : t + 1], scalar2=None, op0=ALU.max)
+
+        def scatter(s):
+            b, t = divmod(s, PACK)
+            nc.vector.tensor_tensor(page[s][:].indirect(list2[:]), h[s][:], wgs_sb[t], ALU.mult)
+
+        def gather(s):
+            b, t = divmod(s, PACK)
+            nc.vector.tensor_copy(x0[b][:, t, :], page[s][:].indirect(list3[:]))
+
+        def round_page(s):
+            b, t = divmod(s, PACK)
+            nc.scalar.copy(out=pairs[b][:, t // 2, :, t % 2], in_=page[s][:])
+
+        def quantize_x0(b, v_share):
+            g = grouped("x0_g%d" % b)
+            dst = g[:].rearrange("p (c i t) -> p c t i", i=PACK, t=PACK)
+            src = x0[b][:].rearrange("p t (c i) -> p c t i", i=PACK)
+            c = v_share // PACK
+            if c:
+                nc.vector.tensor_copy(out=dst[:, :c], in_=src[:, :c])
+            nc.scalar.copy(out=dst[:, c:], in_=src[:, c:])
+            x0_c[b] = shared("h%d" % (4 - 4 * b), [P, NP], U32, "x0_c%d" % b)
+            quantize(x0_c[b][:], x0_s[b][:], g[:])
+
+        page_g = {}
+
+        def weave_page(b, half):
+            words = pairs[b][:].rearrange("p u m e -> p (u m e)").bitcast(F32).rearrange("p (u m) -> p m u", u=2)
+            g = grouped("page_g%d%d" % (b, half))
+            cols = slice(KP * half, KP * (half + 1))
+            nc.scalar.copy(out=g[:].bitcast(F32).rearrange("p (m u) -> p m u", u=2), in_=words[:, cols, :])
+            page_g[b, half] = g
+
+        def quantize_page(b, half):
+            g = page_g[b, half]
+            cols = slice(KP * half, KP * (half + 1))
+            tag = "page_c%d" % half if b else "h%d" % (5 + half)
+            page_c[b, half] = shared(tag, [P, KP], U32, "page_c%d%d" % (b, half))
+            quantize(page_c[b, half][:], page_s[b][:, cols], g[:])
+
+        def prepare_base(half):
+            tile = base_sb[half]
+            for i in range(PACK):
+                col = PACK * half + i
+                nc.scalar.activation(out=tile[:, i, :], in_=tile[:, i, :], func=ACT.Copy, scale=slot_sb[:, col : col + 1])
+
+        first_product(0)
+        floor_h(0)
+        for s in range(SLICES):
+            if s + 1 < SLICES:
+                first_product(s + 1)
+            if s > 0:
+                gather(s - 1)
+            if s + 1 < SLICES:
+                floor_h(s + 1)
+            scatter(s)
+            round_page(s)
+            if s in (1, 2):
+                prepare_w1(s - 1, 1, 0)
+            if s == PACK:
+                quantize_x0(0, 0)
+            if s in (5, 6):
+                weave_page(0, s - 5)
+                quantize_page(0, s - 5)
+            if s in (4, 5):
+                prepare_base(s - 4)
+        gather(SLICES - 1)
+
+        y_acc = [bank(s, "y_acc%d" % s) for s in range(SLICES)]
+
+        def second_product(a):
+            for s in range(SLICES):
+                g = SLICES * a + s
+                nc.tensor.matmul_mx(
+                    out=y_acc[s][:], lhsT=w4_c[:, 2 * P * g : 2 * P * (g + 1)].bitcast(FP4X4),
+                    lhsT_scale=w4_s[:, P * g : P * (g + 1)],
+                    rhs=x0_c[a][:].bitcast(FP8X4), rhs_scale=x0_s[a][:],
+                    start=(a == 0), stop=(a == PASSES - 1),
+                )
+
+        second_product(0)
+        quantize_x0(1, V_SHARE_X0 - 4)
+        second_product(1)
+        x_c = [kept([P, NP], U32, "x_c%d" % b) for b in range(PASSES)]
+        x_s = [kept([P, NP], U8, "x_s%d" % b) for b in range(PASSES)]
+        x_pairs = [kept([P, 2, NP, 2], BF16, "x_pairs%d" % b) for b in range(PASSES)]
+        x_g = {}
+
+        def make_x(s):
+            b, t = divmod(s, PACK)
+            nc.vector.tensor_tensor(x0[b][:, t, :], y_acc[s][:], x0[b][:, t, :], ALU.min)
+            nc.scalar.activation(
+                out=x_pairs[b][:, t // 2, :, t % 2], in_=x0[b][:, t, :], func=ACT.Copy, scale=gain_sb[:, b, t : t + 1]
+            )
+
+        def weave_x(b):
+            x_g[b] = grouped("x_g%d" % b)
+            words = x_pairs[b][:].rearrange("p u m e -> p (u m e)").bitcast(F32).rearrange("p (u m) -> p m u", u=2)
+            nc.vector.tensor_copy(out=x_g[b][:].bitcast(F32).rearrange("p (m u) -> p m u", u=2), in_=words)
+
+        def third_product(b, i):
+            cols = slice(P * i, P * (i + 1))
+            nc.tensor.matmul_mx(
+                out=e_acc[i][:],
+                lhsT=page_c[b, i // PACK][:, P * (i % PACK) : P * (i % PACK + 1)].bitcast(FP8X4),
+                lhsT_scale=page_s[b][:, cols],
+                rhs=x_c[b][:].bitcast(FP8X4), rhs_scale=x_s[b][:],
+                start=(b == 0), stop=(b == PASSES - 1),
+            )
+
+        weave_page(1, 0)
+        weave_page(1, 1)
+        for s in range(5):
+            make_x(s)
+        weave_x(0)
+        make_x(5)
+        quantize(x_c[0][:], x_s[0][:], x_g[0][:])
+        make_x(6)
+        quantize_page(1, 0)
+        make_x(7)
+        quantize_page(1, 1)
+        weave_x(1)
+        quantize(x_c[1][:], x_s[1][:], x_g[1][:])
+        e_acc = [bank(i, "e_acc%d" % i) for i in range(SLICES)]
+        for b in range(PASSES):
+            for i in range(SLICES):
+                third_product(b, i)
+        for i in range(SLICES):
+            res = base_sb[i // PACK][:, i % PACK, :]
+            nc.vector.scalar_tensor_tensor(
+                out=res, in0=e_acc[i][:], scalar=slot_sb[:, i : i + 1], in1=res, op0=ALU.mult, op1=ALU.subtract
+            )
+            nc.sync.dma_start(out=out[P * i : P * (i + 1), :], in_=res)

@@ -21,8 +21,7 @@ PACK = 4
 KP = 512
 PASSES = 2
 SLICES = 8
-V_SHARE_W1 = 84
-V_SHARE_X0 = 340
+F32_MAX = 3.4028234663852886e38
 
 
 def tile_list_salt_pond_readout_kernel(
@@ -40,9 +39,6 @@ def tile_list_salt_pond_readout_kernel(
 
         def shared(tag, shape, dtype, name):
             return ring.tile(shape, dtype, name=name, tag=tag, bufs=1, align_bytes=64)
-
-        def big(name):
-            return ring.tile([P, PACK, KP], F32, name=name, tag="big", bufs=4, align_bytes=64)
 
         def grouped(name):
             return ring.tile([P, KP * PACK], BF16, name=name, tag="grouped", bufs=4, align_bytes=64)
@@ -68,7 +64,7 @@ def tile_list_salt_pond_readout_kernel(
             nc.sync.dma_start(out=tab_w[a][:], in_=tab_words[a].rearrange("p t i -> p (t i)").bitcast(I32))
 
         def load_w1(a, b):
-            w1_raw[a, b] = big("w1_raw%d%d" % (a, b))
+            w1_raw[a, b] = shared("w1_raw%d%d" % (a, b), [P, PACK, KP], F32, "w1_raw%d%d" % (a, b))
             nc.sync.dma_start(
                 out=w1_raw[a, b][:],
                 in_=w1[KP * a : KP * (a + 1), KP * b : KP * (b + 1)].rearrange("(p j) c -> p j c", j=PACK),
@@ -116,7 +112,7 @@ def tile_list_salt_pond_readout_kernel(
 
         season_rows = season.rearrange("(b p t) j -> b t p j", b=PASSES, t=PACK)
         page_rows = page0.rearrange("(b p t) m -> b t p m", b=PASSES, t=PACK)
-        season_sb = [kept([P, S], F32, "season%d" % s) for s in range(SLICES)]
+        h = [shared("h%d" % s, [P, S], F32, "h%d" % s) for s in range(SLICES)]
         page = [kept([P, T2], F32, "page%d" % s) for s in range(SLICES)]
         wgs_first = kept([P, 1, S], F32, "wgs_first")
         wgs_rest = kept([P, PACK - 1, S], F32, "wgs_rest")
@@ -124,7 +120,7 @@ def tile_list_salt_pond_readout_kernel(
         wgs_sb = [wgs_first[:, 0, :]] + [wgs_rest[:, t, :] for t in range(PACK - 1)]
 
         def load_season(s):
-            nc.sync.dma_start(out=season_sb[s][:], in_=season_rows[s // PACK, s % PACK])
+            nc.sync.dma_start(out=h[s][:], in_=season_rows[s // PACK, s % PACK])
 
         def load_page(s):
             nc.sync.dma_start(out=page[s][:], in_=page_rows[s // PACK, s % PACK])
@@ -147,9 +143,9 @@ def tile_list_salt_pond_readout_kernel(
         nc.sync.dma_start(list3[:], offs3)
         for q in range(4):
             nc.sync.dma_start(out=wgs_rest[32 * q : 32 * q + 32, :, :], in_=wgs_rows[:, 1:PACK, :])
-        load_page(1)
-        load_w1(0, 1)
         load_season(2)
+        load_w1(0, 1)
+        load_page(1)
         load_w1(1, 1)
         load_season(3)
         load_page(2)
@@ -168,50 +164,66 @@ def tile_list_salt_pond_readout_kernel(
 
         w1_c, w1_s = {}, {}
 
-        def prepare_w1(a, b, v_share):
-            g = grouped("w1_g%d%d" % (a, b))
-            dst = g[:].rearrange("p (t m j) -> p m j t", t=PACK, j=PACK)
-            src = w1_raw[a, b][:].rearrange("p j (m t) -> p m j t", t=PACK)
-            if v_share:
-                nc.vector.tensor_copy(out=dst[:, :v_share], in_=src[:, :v_share])
-            nc.scalar.copy(out=dst[:, v_share:], in_=src[:, v_share:])
+        w1_g = {}
+
+        def weave_w1(a, b):
+            w1_g[a, b] = grouped("w1_g%d%d" % (a, b))
+            nc.scalar.copy(
+                out=w1_g[a, b][:].rearrange("p (t m j) -> p m j t", t=PACK, j=PACK),
+                in_=w1_raw[a, b][:].rearrange("p j (m t) -> p m j t", t=PACK),
+            )
+
+        def quantize_w1(a, b):
             w1_c[a, b] = shared("h%d" % (a + 1) if b else "w1_c%d" % a, [P, KP], U32, "w1_c%d%d" % (a, b))
             w1_s[a, b] = kept([P, KP], U8, "w1_s%d%d" % (a, b))
-            quantize(w1_c[a, b][:], w1_s[a, b][:], g[:])
+            quantize(w1_c[a, b][:], w1_s[a, b][:], w1_g[a, b][:])
 
-        prepare_w1(0, 0, 0)
-        prepare_w1(1, 0, 0)
+        for a in range(PASSES):
+            weave_w1(a, 0)
+            quantize_w1(a, 0)
 
         x0 = [kept([P, PACK, NP], F32, "x0_%d" % b) for b in range(PASSES)]
-        pairs = [kept([P, 2, T2, 2], BF16, "pairs%d" % b) for b in range(PASSES)]
+        pairs = {1: kept([P, 2, T2, 2], BF16, "pairs1")}
         x0_c, page_c = {}, {}
         x0_s = [kept([P, NP], U8, "x0_s%d" % b) for b in range(PASSES)]
         page_s = [kept([P, T2], U8, "page_s%d" % b) for b in range(PASSES)]
-        h = {}
+        acc = {}
 
         def first_product(s):
             b, t = divmod(s, PACK)
-            acc = bank(s, "h_acc%d" % s)
+            acc[s] = bank(s, "h_acc%d" % s)
             cols = slice(P * t, P * (t + 1))
             for a in range(PASSES):
                 nc.tensor.matmul_mx(
-                    out=acc[:], lhsT=w1_c[a, b][:, cols].bitcast(FP8X4), lhsT_scale=w1_s[a, b][:, cols],
+                    out=acc[s][:], lhsT=w1_c[a, b][:, cols].bitcast(FP8X4), lhsT_scale=w1_s[a, b][:, cols],
                     rhs=v_c[a][:].bitcast(FP8X4), rhs_scale=v_s[4 * a : P, :],
                     start=(a == 0), stop=(a == PASSES - 1),
                 )
-            h[s] = shared("h%d" % s, [P, S], F32, "h%d" % s)
+
+        def features_on_vector(s):
+            b, t = divmod(s, PACK)
             nc.vector.scalar_tensor_tensor(
-                out=h[s][:], in0=acc[:], scalar=cap_sb[:, b, t : t + 1], in1=season_sb[s][:],
-                op0=ALU.min, op1=ALU.add,
+                out=h[s][:], in0=acc[s][:], scalar=cap_sb[:, b, t : t + 1], in1=h[s][:], op0=ALU.min, op1=ALU.add
+            )
+            nc.vector.scalar_tensor_tensor(
+                out=h[s][:], in0=h[s][:], scalar=low_sb[:, b, t : t + 1], in1=wgs_sb[t], op0=ALU.max, op1=ALU.mult
             )
 
-        def floor_h(s):
+        def features_off_vector(s):
             b, t = divmod(s, PACK)
-            nc.vector.tensor_scalar(out=h[s][:], in0=h[s][:], scalar1=low_sb[:, b, t : t + 1], scalar2=None, op0=ALU.max)
+            room = ring.tile([P, S], F32, name="room%d" % s, tag="room", bufs=4, align_bytes=64)
+            nc.scalar.activation(out=room[:], in_=acc[s][:], func=ACT.Relu, scale=-1.0, bias=cap_sb[:, b, t : t + 1])
+            nc.gpsimd.tensor_scalar(
+                out=h[s][:], in0=h[s][:], scalar1=cap_sb[:, b, t : t + 1], scalar2=1.0, op0=ALU.add, op1=ALU.mult
+            )
+            nc.gpsimd.tensor_tensor(h[s][:], h[s][:], room[:], ALU.subtract)
+            nc.gpsimd.tensor_scalar(
+                out=h[s][:], in0=h[s][:], scalar1=F32_MAX, scalar2=low_sb[:, b, t : t + 1], op0=ALU.min, op1=ALU.max
+            )
+            nc.gpsimd.tensor_tensor(h[s][:], h[s][:], wgs_sb[t], ALU.mult)
 
         def scatter(s):
-            b, t = divmod(s, PACK)
-            nc.vector.tensor_tensor(page[s][:].indirect(list2[:]), h[s][:], wgs_sb[t], ALU.mult)
+            nc.vector.tensor_copy(page[s][:].indirect(list2[:]), h[s][:])
 
         def gather(s):
             b, t = divmod(s, PACK)
@@ -228,7 +240,8 @@ def tile_list_salt_pond_readout_kernel(
             c = v_share // PACK
             if c:
                 nc.vector.tensor_copy(out=dst[:, :c], in_=src[:, :c])
-            nc.scalar.copy(out=dst[:, c:], in_=src[:, c:])
+            else:
+                nc.scalar.copy(out=dst, in_=src)
             x0_c[b] = shared("h%d" % (4 - 4 * b), [P, NP], U32, "x0_c%d" % b)
             quantize(x0_c[b][:], x0_s[b][:], g[:])
 
@@ -252,29 +265,37 @@ def tile_list_salt_pond_readout_kernel(
             tile = base_sb[half]
             for i in range(PACK):
                 col = PACK * half + i
-                nc.scalar.activation(out=tile[:, i, :], in_=tile[:, i, :], func=ACT.Copy, scale=slot_sb[:, col : col + 1])
+                nc.gpsimd.tensor_scalar(
+                    out=tile[:, i, :], in0=tile[:, i, :], scalar1=slot_sb[:, col : col + 1], scalar2=0.0,
+                    op0=ALU.mult, op1=ALU.add,
+                )
 
         first_product(0)
-        floor_h(0)
+        features_on_vector(0)
+        for s in range(1, PACK):
+            first_product(s)
+            features_off_vector(s)
         for s in range(SLICES):
-            if s + 1 < SLICES:
-                first_product(s + 1)
-            if s > 0:
-                gather(s - 1)
-            if s + 1 < SLICES:
-                floor_h(s + 1)
             scatter(s)
-            round_page(s)
-            if s in (1, 2):
-                prepare_w1(s - 1, 1, 0)
+            if s == 2:
+                for a in range(PASSES):
+                    quantize_w1(a, 1)
+                for later in range(PACK, SLICES):
+                    first_product(later)
+                    features_off_vector(later)
             if s == PACK:
                 quantize_x0(0, 0)
             if s in (5, 6):
                 weave_page(0, s - 5)
                 quantize_page(0, s - 5)
+            gather(s)
+            if s == 0:
+                for a in range(PASSES):
+                    weave_w1(a, 1)
+                pairs[0] = shared("w1_raw11", [P, 2, T2, 2], BF16, "pairs0")
+            round_page(s)
             if s in (4, 5):
                 prepare_base(s - 4)
-        gather(SLICES - 1)
 
         y_acc = [bank(s, "y_acc%d" % s) for s in range(SLICES)]
 
@@ -289,7 +310,7 @@ def tile_list_salt_pond_readout_kernel(
                 )
 
         second_product(0)
-        quantize_x0(1, V_SHARE_X0 - 4)
+        quantize_x0(1, NP)
         second_product(1)
         x_c = [kept([P, NP], U32, "x_c%d" % b) for b in range(PASSES)]
         x_s = [kept([P, NP], U8, "x_s%d" % b) for b in range(PASSES)]

@@ -22,6 +22,7 @@ KP = 512
 PASSES = 2
 SLICES = 8
 F32_MAX = 3.4028234663852886e38
+H_SLOT = ("h_a", "h_b", "h_a", "g_w1", "h_c", "g_w1", "h_c", "g_w1")
 
 
 def tile_list_salt_pond_readout_kernel(
@@ -40,8 +41,10 @@ def tile_list_salt_pond_readout_kernel(
         def shared(tag, shape, dtype, name):
             return ring.tile(shape, dtype, name=name, tag=tag, bufs=1, align_bytes=64)
 
-        def grouped(name):
-            return ring.tile([P, KP * PACK], BF16, name=name, tag="grouped", bufs=4, align_bytes=64)
+        def grouped(name, tag=None):
+            if tag:
+                return shared(tag, [P, KP * PACK], BF16, name)
+            return ring.tile([P, KP * PACK], BF16, name=name, tag="grouped", bufs=5, align_bytes=64)
 
         def bank(i, name):
             return psum.tile([P, KP], F32, name=name, tag="bank%d" % i)
@@ -112,7 +115,7 @@ def tile_list_salt_pond_readout_kernel(
 
         season_rows = season.rearrange("(b p t) j -> b t p j", b=PASSES, t=PACK)
         page_rows = page0.rearrange("(b p t) m -> b t p m", b=PASSES, t=PACK)
-        h = [shared("h%d" % s, [P, S], F32, "h%d" % s) for s in range(SLICES)]
+        season_sb = [kept([P, S], F32, "season%d" % s) for s in range(SLICES)]
         page = [kept([P, T2], F32, "page%d" % s) for s in range(SLICES)]
         wgs_first = kept([P, 1, S], F32, "wgs_first")
         wgs_rest = kept([P, PACK - 1, S], F32, "wgs_rest")
@@ -120,7 +123,7 @@ def tile_list_salt_pond_readout_kernel(
         wgs_sb = [wgs_first[:, 0, :]] + [wgs_rest[:, t, :] for t in range(PACK - 1)]
 
         def load_season(s):
-            nc.sync.dma_start(out=h[s][:], in_=season_rows[s // PACK, s % PACK])
+            nc.sync.dma_start(out=season_sb[s][:], in_=season_rows[s // PACK, s % PACK])
 
         def load_page(s):
             nc.sync.dma_start(out=page[s][:], in_=page_rows[s // PACK, s % PACK])
@@ -167,14 +170,14 @@ def tile_list_salt_pond_readout_kernel(
         w1_g = {}
 
         def weave_w1(a, b):
-            w1_g[a, b] = grouped("w1_g%d%d" % (a, b))
+            w1_g[a, b] = grouped("w1_g%d%d" % (a, b), "g_w1" if (a, b) == (0, 1) else None)
             nc.scalar.copy(
                 out=w1_g[a, b][:].rearrange("p (t m j) -> p m j t", t=PACK, j=PACK),
                 in_=w1_raw[a, b][:].rearrange("p j (m t) -> p m j t", t=PACK),
             )
 
         def quantize_w1(a, b):
-            w1_c[a, b] = shared("h%d" % (a + 1) if b else "w1_c%d" % a, [P, KP], U32, "w1_c%d%d" % (a, b))
+            w1_c[a, b] = shared(H_SLOT[1 + a] if b else "w1_c%d" % a, [P, KP], U32, "w1_c%d%d" % (a, b))
             w1_s[a, b] = kept([P, KP], U8, "w1_s%d%d" % (a, b))
             quantize(w1_c[a, b][:], w1_s[a, b][:], w1_g[a, b][:])
 
@@ -182,7 +185,7 @@ def tile_list_salt_pond_readout_kernel(
             weave_w1(a, 0)
             quantize_w1(a, 0)
 
-        x0 = [kept([P, PACK, NP], F32, "x0_%d" % b) for b in range(PASSES)]
+        x0 = [shared("x0_%d" % b, [P, PACK, NP], F32, "x0_%d" % b) for b in range(PASSES)]
         pairs = {1: kept([P, 2, T2, 2], BF16, "pairs1")}
         x0_c, page_c = {}, {}
         x0_s = [kept([P, NP], U8, "x0_s%d" % b) for b in range(PASSES)]
@@ -200,23 +203,31 @@ def tile_list_salt_pond_readout_kernel(
                     start=(a == 0), stop=(a == PASSES - 1),
                 )
 
+        h, room = {}, {}
+
         def features_on_vector(s):
             b, t = divmod(s, PACK)
+            capped = shared(H_SLOT[s + 1], [P, S], F32, "capped")
             nc.vector.scalar_tensor_tensor(
-                out=h[s][:], in0=acc[s][:], scalar=cap_sb[:, b, t : t + 1], in1=h[s][:], op0=ALU.min, op1=ALU.add
+                out=capped[:], in0=acc[s][:], scalar=cap_sb[:, b, t : t + 1], in1=season_sb[s][:],
+                op0=ALU.min, op1=ALU.add,
             )
+            h[s] = shared(H_SLOT[s], [P, S], F32, "h%d" % s)
             nc.vector.scalar_tensor_tensor(
-                out=h[s][:], in0=h[s][:], scalar=low_sb[:, b, t : t + 1], in1=wgs_sb[t], op0=ALU.max, op1=ALU.mult
+                out=h[s][:], in0=capped[:], scalar=low_sb[:, b, t : t + 1], in1=wgs_sb[t], op0=ALU.max, op1=ALU.mult
             )
 
-        def features_off_vector(s):
+        def features_on_scalar(s):
             b, t = divmod(s, PACK)
-            room = ring.tile([P, S], F32, name="room%d" % s, tag="room", bufs=4, align_bytes=64)
-            nc.scalar.activation(out=room[:], in_=acc[s][:], func=ACT.Relu, scale=-1.0, bias=cap_sb[:, b, t : t + 1])
-            nc.gpsimd.tensor_scalar(
-                out=h[s][:], in0=h[s][:], scalar1=cap_sb[:, b, t : t + 1], scalar2=1.0, op0=ALU.add, op1=ALU.mult
-            )
-            nc.gpsimd.tensor_tensor(h[s][:], h[s][:], room[:], ALU.subtract)
+            cap_col = cap_sb[:, b, t : t + 1]
+            room[s] = ring.tile([P, S], F32, name="room%d" % s, tag="room", bufs=4, align_bytes=64)
+            nc.scalar.activation(out=room[s][:], in_=acc[s][:], func=ACT.Relu, scale=-1.0, bias=cap_col)
+            nc.scalar.activation(out=season_sb[s][:], in_=season_sb[s][:], func=ACT.Identity, bias=cap_col)
+
+        def features_on_gpsimd(s):
+            b, t = divmod(s, PACK)
+            h[s] = shared(H_SLOT[s], [P, S], F32, "h%d" % s)
+            nc.gpsimd.tensor_tensor(h[s][:], season_sb[s][:], room[s][:], ALU.subtract)
             nc.gpsimd.tensor_scalar(
                 out=h[s][:], in0=h[s][:], scalar1=F32_MAX, scalar2=low_sb[:, b, t : t + 1], op0=ALU.min, op1=ALU.max
             )
@@ -233,7 +244,9 @@ def tile_list_salt_pond_readout_kernel(
             b, t = divmod(s, PACK)
             nc.scalar.copy(out=pairs[b][:, t // 2, :, t % 2], in_=page[s][:])
 
-        def quantize_x0(b, v_share):
+        x0_g = {}
+
+        def weave_x0(b, v_share):
             g = grouped("x0_g%d" % b)
             dst = g[:].rearrange("p (c i t) -> p c t i", i=PACK, t=PACK)
             src = x0[b][:].rearrange("p t (c i) -> p c t i", i=PACK)
@@ -242,8 +255,7 @@ def tile_list_salt_pond_readout_kernel(
                 nc.vector.tensor_copy(out=dst[:, :c], in_=src[:, :c])
             else:
                 nc.scalar.copy(out=dst, in_=src)
-            x0_c[b] = shared("h%d" % (4 - 4 * b), [P, NP], U32, "x0_c%d" % b)
-            quantize(x0_c[b][:], x0_s[b][:], g[:])
+            x0_g[b] = g
 
         page_g = {}
 
@@ -257,45 +269,40 @@ def tile_list_salt_pond_readout_kernel(
         def quantize_page(b, half):
             g = page_g[b, half]
             cols = slice(KP * half, KP * (half + 1))
-            tag = "page_c%d" % half if b else "h%d" % (5 + half)
-            page_c[b, half] = shared(tag, [P, KP], U32, "page_c%d%d" % (b, half))
-            quantize(page_c[b, half][:], page_s[b][:, cols], g[:])
-
-        def prepare_base(half):
-            tile = base_sb[half]
-            for i in range(PACK):
-                col = PACK * half + i
-                nc.gpsimd.tensor_scalar(
-                    out=tile[:, i, :], in0=tile[:, i, :], scalar1=slot_sb[:, col : col + 1], scalar2=0.0,
-                    op0=ALU.mult, op1=ALU.add,
-                )
+            quantize(page_c[b, half], page_s[b][:, cols], g[:])
 
         first_product(0)
         features_on_vector(0)
         for s in range(1, PACK):
             first_product(s)
-            features_off_vector(s)
+            features_on_scalar(s)
+        features_on_gpsimd(1)
         for s in range(SLICES):
             scatter(s)
-            if s == 2:
-                for a in range(PASSES):
-                    quantize_w1(a, 1)
-                for later in range(PACK, SLICES):
-                    first_product(later)
-                    features_off_vector(later)
-            if s == PACK:
-                quantize_x0(0, 0)
-            if s in (5, 6):
-                weave_page(0, s - 5)
-                quantize_page(0, s - 5)
-            gather(s)
             if s == 0:
                 for a in range(PASSES):
                     weave_w1(a, 1)
                 pairs[0] = shared("w1_raw11", [P, 2, T2, 2], BF16, "pairs0")
+            if s in (1, 2):
+                quantize_w1(s - 1, 1)
+            if s == 2:
+                for later in range(PACK, SLICES):
+                    first_product(later)
+                    features_on_scalar(later)
+            if s == PACK:
+                weave_x0(0, 0)
+                weave_page(0, 0)
+                weave_page(0, 1)
+            if s == 6:
+                late = shared(H_SLOT[s], [P, 3, KP], U32, "late_codes")
+                x0_c[0], page_c[0, 0], page_c[0, 1] = late[:, 0, :], late[:, 1, :], late[:, 2, :]
+                quantize(x0_c[0], x0_s[0][:], x0_g[0][:])
+                quantize_page(0, 0)
+                quantize_page(0, 1)
+            gather(s)
             round_page(s)
-            if s in (4, 5):
-                prepare_base(s - 4)
+            if s + 2 < SLICES:
+                features_on_gpsimd(s + 2)
 
         y_acc = [bank(s, "y_acc%d" % s) for s in range(SLICES)]
 
@@ -305,16 +312,19 @@ def tile_list_salt_pond_readout_kernel(
                 nc.tensor.matmul_mx(
                     out=y_acc[s][:], lhsT=w4_c[:, 2 * P * g : 2 * P * (g + 1)].bitcast(FP4X4),
                     lhsT_scale=w4_s[:, P * g : P * (g + 1)],
-                    rhs=x0_c[a][:].bitcast(FP8X4), rhs_scale=x0_s[a][:],
+                    rhs=x0_c[a].bitcast(FP8X4), rhs_scale=x0_s[a][:],
                     start=(a == 0), stop=(a == PASSES - 1),
                 )
 
         second_product(0)
-        quantize_x0(1, NP)
+        weave_x0(1, NP)
+        last = kept([P, 3, KP], U32, "last_codes")
+        x0_c[1], page_c[1, 0], page_c[1, 1] = last[:, 0, :], last[:, 1, :], last[:, 2, :]
+        quantize(x0_c[1], x0_s[1][:], x0_g[1][:])
         second_product(1)
         x_c = [kept([P, NP], U32, "x_c%d" % b) for b in range(PASSES)]
         x_s = [kept([P, NP], U8, "x_s%d" % b) for b in range(PASSES)]
-        x_pairs = [kept([P, 2, NP, 2], BF16, "x_pairs%d" % b) for b in range(PASSES)]
+        x_pairs = [shared("x_pairs%d" % b, [P, 2, NP, 2], BF16, "x_pairs%d" % b) for b in range(PASSES)]
         x_g = {}
 
         def make_x(s):
@@ -356,8 +366,14 @@ def tile_list_salt_pond_readout_kernel(
         for b in range(PASSES):
             for i in range(SLICES):
                 third_product(b, i)
+        scored = [shared(tag, [P, PACK, NP], F32, "scored_" + tag) for tag in ("x0_1", "x_pairs1")]
         for i in range(SLICES):
-            res = base_sb[i // PACK][:, i % PACK, :]
+            nc.scalar.activation(
+                out=scored[i // PACK][:, i % PACK, :], in_=base_sb[i // PACK][:, i % PACK, :],
+                func=ACT.Copy, scale=slot_sb[:, i : i + 1],
+            )
+        for i in range(SLICES):
+            res = scored[i // PACK][:, i % PACK, :]
             nc.vector.scalar_tensor_tensor(
                 out=res, in0=e_acc[i][:], scalar=slot_sb[:, i : i + 1], in1=res, op0=ALU.mult, op1=ALU.subtract
             )

from contextlib import ExitStack

import concourse.mybir as mybir

K, H, T, S, T2, NP = 1024, 1024, 2048, 512, 1024, 512
FLOPS = 2 * K * H * S + 2 * H * H * NP + 2 * H * T2 * NP

F32 = mybir.dt.float32
BF16 = mybir.dt.bfloat16
I32 = mybir.dt.int32
U32 = mybir.dt.uint32
U16 = mybir.dt.uint16
U8 = mybir.dt.uint8
FP8X4 = mybir.dt.float8_e4m3fn_x4
FP4X4 = mybir.dt.float4_e2m1fn_x4
ALU = mybir.AluOpType
ACT = mybir.ActivationFunctionType

P = 128
PACK = 4
KP = 512
PASSES = 2
SLICES = 8
F32_MAX = 3.4028234663852886e38
H_SLOT = ("h_a", "h_b", "h_a", "g_w1", "h_c", "g_w1", "h_c", "g_w1")


def tile_list_salt_pond_readout_kernel(
    tc, tab_words, tab_scales, offs, w1, cap, season, low, wgs, page0, offs2, offs3,
    w4_words, w4_scales, gain, base, slot, out,
):
    nc = tc.nc
    with ExitStack() as ctx:
        keep = ctx.enter_context(tc.tile_pool(name="keep", bufs=1))
        ring = ctx.enter_context(tc.tile_pool(name="ring", bufs=1))
        psum = ctx.enter_context(tc.psum_pool(name="psum", bufs=1))

        def kept(shape, dtype, name):
            return keep.tile(shape, dtype, name=name, align_bytes=64)

        def shared(tag, shape, dtype, name):
            return ring.tile(shape, dtype, name=name, tag=tag, bufs=1, align_bytes=64)

        def grouped(name, tag=None):
            if tag:
                return shared(tag, [P, KP * PACK], BF16, name)
            return ring.tile([P, KP * PACK], BF16, name=name, tag="grouped", bufs=5, align_bytes=64)

        def bank(i, name):
            return psum.tile([P, KP], F32, name=name, tag="bank%d" % i)

        list1 = kept([P, S // 16], U16, "list1")
        list2 = kept([P, S // 16], U16, "list2")
        list3 = kept([P, NP // 16], U16, "list3")

        tab_sc = kept([P, T], U8, "tab_sc")
        w4_sc_raw = kept([P, PASSES, H], U8, "w4_sc_raw")
        nc.vector.memset(w4_sc_raw[:].rearrange("p a n -> p (a n)").bitcast(I32), 0)
        nc.vector.memset(tab_sc[:].bitcast(I32), 0)

        w4_raw = kept([P, PASSES, 2 * H], U8, "w4_raw")
        nc.sync.dma_start(out=w4_raw[:].bitcast(I32), in_=w4_words.rearrange("a p n -> p a n").bitcast(I32))
        tab_w = [shared("tab%d" % a, [P, T], I32, "tab_w%d" % a) for a in range(PASSES)]
        w1_raw = {}

        def load_tab(a):
            nc.sync.dma_start(out=tab_w[a][:], in_=tab_words[a].rearrange("p t i -> p (t i)").bitcast(I32))

        def load_w1(a, b):
            w1_raw[a, b] = shared("w1_raw%d%d" % (a, b), [P, PACK, KP], F32, "w1_raw%d%d" % (a, b))
            nc.sync.dma_start(
                out=w1_raw[a, b][:],
                in_=w1[KP * a : KP * (a + 1), KP * b : KP * (b + 1)].rearrange("(p j) c -> p j c", j=PACK),
            )

        for q in range(4):
            nc.sync.dma_start(
                out=w4_sc_raw[32 * q : 32 * q + 4, :, :].bitcast(I32),
                in_=w4_scales[:, 4 * q : 4 * q + 4, :].rearrange("a r n -> r a n").bitcast(I32),
            )
        load_w1(0, 0)
        nc.sync.dma_start(list1[:], offs)
        load_w1(1, 0)
        for q in range(4):
            nc.sync.dma_start(
                out=tab_sc[32 * q : 32 * q + 8, :].bitcast(I32),
                in_=tab_scales[:, 4 * q : 4 * q + 4, :].bitcast(I32),
            )
        cap_sb = kept([P, PASSES, PACK], F32, "cap_sb")
        low_sb = kept([P, PASSES, PACK], F32, "low_sb")
        gain_sb = kept([P, PASSES, PACK], F32, "gain_sb")
        slot_sb = kept([P, SLICES], F32, "slot_sb")
        load_tab(0)
        load_tab(1)
        nc.gpsimd.dma_start(out=cap_sb[:], in_=cap.rearrange("(b p t) -> p b t", b=PASSES, t=PACK))
        nc.gpsimd.dma_start(out=low_sb[:], in_=low.rearrange("(b p t) -> p b t", b=PASSES, t=PACK))

        w4_c = kept([P, PASSES * 2 * H], U8, "w4_c")
        w4_s = kept([P, PASSES * H], U8, "w4_s")
        nc.vector.tensor_copy(
            out=w4_c[:].bitcast(U16).rearrange("p (g t q) -> p g q t", t=PACK, q=P),
            in_=w4_raw[:].rearrange("p a n -> p (a n)").bitcast(U16).rearrange("p (g q t) -> p g q t", t=PACK, q=P),
        )

        nc.vector.tensor_copy(
            out=w4_s[:].rearrange("p (g t q) -> p g q t", t=PACK, q=P),
            in_=w4_sc_raw[:].rearrange("p a n -> p (a n)").rearrange("p (g q t) -> p g q t", t=PACK, q=P),
        )

        v_s = kept([P, S], U8, "v_s")
        v_c = [kept([P, S], U32, "v_c%d" % a) for a in range(PASSES)]
        nc.vector.tensor_copy(v_s[:], tab_sc[:].indirect(list1[:]))
        nc.vector.tensor_copy(v_c[0][:], tab_w[0][:].bitcast(U32).indirect(list1[:]))
        nc.vector.tensor_copy(v_c[1][:], tab_w[1][:].bitcast(U32).indirect(list1[:]))

        season_rows = season.rearrange("(b p t) j -> b t p j", b=PASSES, t=PACK)
        page_rows = page0.rearrange("(b p t) m -> b t p m", b=PASSES, t=PACK)
        season_sb = [kept([P, S], F32, "season%d" % s) for s in range(SLICES)]
        page = [kept([P, T2], F32, "page%d" % s) for s in range(SLICES)]
        wgs_first = kept([P, 1, S], F32, "wgs_first")
        wgs_rest = kept([P, PACK - 1, S], F32, "wgs_rest")
        wgs_rows = wgs.rearrange("(p t) j -> p t j", t=PACK)
        wgs_sb = [wgs_first[:, 0, :]] + [wgs_rest[:, t, :] for t in range(PACK - 1)]

        def load_season(s):
            nc.sync.dma_start(out=season_sb[s][:], in_=season_rows[s // PACK, s % PACK])

        def load_page(s):
            nc.sync.dma_start(out=page[s][:], in_=page_rows[s // PACK, s % PACK])

        base_sb = []

        def load_base(half):
            tile = shared("tab%d" % half, [P, PACK, NP], F32, "base%d" % half)
            base_sb.append(tile)
            nc.sync.dma_start(
                out=tile[:], in_=base[KP * half : KP * (half + 1), :].rearrange("(i p) j -> p i j", p=P)
            )

        nc.sync.dma_start(list2[:], offs2)
        load_season(0)
        for q in range(4):
            nc.sync.dma_start(out=wgs_first[32 * q : 32 * q + 32, :, :], in_=wgs_rows[:, 0:1, :])
        load_page(0)
        load_season(1)
        nc.sync.dma_start(list3[:], offs3)
        for q in range(4):
            nc.sync.dma_start(out=wgs_rest[32 * q : 32 * q + 32, :, :], in_=wgs_rows[:, 1:PACK, :])
        load_season(2)
        load_w1(0, 1)
        load_page(1)
        load_w1(1, 1)
        load_season(3)
        load_page(2)
        nc.sync.dma_start(out=gain_sb[:], in_=gain.rearrange("(b p t) -> p b t", b=PASSES, t=PACK))
        with nc.allow_non_contiguous_dma(reason="one value of slot for each output row"):
            nc.sync.dma_start(out=slot_sb[:], in_=slot.rearrange("(i p) -> p i", p=P))
        for s in range(3, SLICES):
            if s + 1 < SLICES:
                load_season(s + 1)
            load_page(s)
            if s in (4, 5):
                load_base(s - 4)

        def quantize(codes, scales, src):
            nc.vector.quantize_mx(out=codes.bitcast(FP8X4), scales=scales, in_=src)

        w1_c, w1_s = {}, {}

        w1_g = {}

        def weave_w1(a, b):
            w1_g[a, b] = grouped("w1_g%d%d" % (a, b), "g_w1" if (a, b) == (0, 1) else None)
            nc.scalar.copy(
                out=w1_g[a, b][:].rearrange("p (t m j) -> p m j t", t=PACK, j=PACK),
                in_=w1_raw[a, b][:].rearrange("p j (m t) -> p m j t", t=PACK),
            )

        def quantize_w1(a, b):
            w1_c[a, b] = shared(H_SLOT[1 + a] if b else "w1_c%d" % a, [P, KP], U32, "w1_c%d%d" % (a, b))
            w1_s[a, b] = kept([P, KP], U8, "w1_s%d%d" % (a, b))
            quantize(w1_c[a, b][:], w1_s[a, b][:], w1_g[a, b][:])

        for a in range(PASSES):
            weave_w1(a, 0)
            quantize_w1(a, 0)

        x0 = [shared("x0_%d" % b, [P, PACK, NP], F32, "x0_%d" % b) for b in range(PASSES)]
        pairs = {1: kept([P, 2, T2, 2], BF16, "pairs1")}
        x0_c, page_c = {}, {}
        x0_s = [kept([P, NP], U8, "x0_s%d" % b) for b in range(PASSES)]
        page_s = [kept([P, T2], U8, "page_s%d" % b) for b in range(PASSES)]
        acc = {}

        def first_product(s):
            b, t = divmod(s, PACK)
            acc[s] = bank(s, "h_acc%d" % s)
            cols = slice(P * t, P * (t + 1))
            for a in range(PASSES):
                nc.tensor.matmul_mx(
                    out=acc[s][:], lhsT=w1_c[a, b][:, cols].bitcast(FP8X4), lhsT_scale=w1_s[a, b][:, cols],
                    rhs=v_c[a][:].bitcast(FP8X4), rhs_scale=v_s[4 * a : P, :],
                    start=(a == 0), stop=(a == PASSES - 1),
                )

        h, room = {}, {}

        def features_on_vector(s):
            b, t = divmod(s, PACK)
            capped = shared(H_SLOT[s + 1], [P, S], F32, "capped")
            nc.vector.scalar_tensor_tensor(
                out=capped[:], in0=acc[s][:], scalar=cap_sb[:, b, t : t + 1], in1=season_sb[s][:],
                op0=ALU.min, op1=ALU.add,
            )
            h[s] = shared(H_SLOT[s], [P, S], F32, "h%d" % s)
            nc.vector.scalar_tensor_tensor(
                out=h[s][:], in0=capped[:], scalar=low_sb[:, b, t : t + 1], in1=wgs_sb[t], op0=ALU.max, op1=ALU.mult
            )

        def features_on_scalar(s):
            b, t = divmod(s, PACK)
            cap_col = cap_sb[:, b, t : t + 1]
            room[s] = ring.tile([P, S], F32, name="room%d" % s, tag="room", bufs=4, align_bytes=64)
            nc.scalar.activation(out=room[s][:], in_=acc[s][:], func=ACT.Relu, scale=-1.0, bias=cap_col)
            nc.scalar.activation(out=season_sb[s][:], in_=season_sb[s][:], func=ACT.Identity, bias=cap_col)

        def features_on_gpsimd(s):
            b, t = divmod(s, PACK)
            h[s] = shared(H_SLOT[s], [P, S], F32, "h%d" % s)
            nc.gpsimd.tensor_tensor(h[s][:], season_sb[s][:], room[s][:], ALU.subtract)
            nc.gpsimd.tensor_scalar(
                out=h[s][:], in0=h[s][:], scalar1=F32_MAX, scalar2=low_sb[:, b, t : t + 1], op0=ALU.min, op1=ALU.max
            )
            nc.gpsimd.tensor_tensor(h[s][:], h[s][:], wgs_sb[t], ALU.mult)

        def scatter(s):
            nc.vector.tensor_copy(page[s][:].indirect(list2[:]), h[s][:])

        def gather(s):
            b, t = divmod(s, PACK)
            nc.vector.tensor_copy(x0[b][:, t, :], page[s][:].indirect(list3[:]))

        def round_page(s):
            b, t = divmod(s, PACK)
            nc.scalar.copy(out=pairs[b][:, t // 2, :, t % 2], in_=page[s][:])

        x0_g = {}

        def weave_x0(b, v_share):
            g = grouped("x0_g%d" % b)
            dst = g[:].rearrange("p (c i t) -> p c t i", i=PACK, t=PACK)
            src = x0[b][:].rearrange("p t (c i) -> p c t i", i=PACK)
            c = v_share // PACK
            if c:
                nc.vector.tensor_copy(out=dst[:, :c], in_=src[:, :c])
            else:
                nc.scalar.copy(out=dst, in_=src)
            x0_g[b] = g

        page_g = {}

        def weave_page(b, half):
            words = pairs[b][:].rearrange("p u m e -> p (u m e)").bitcast(F32).rearrange("p (u m) -> p m u", u=2)
            g = grouped("page_g%d%d" % (b, half))
            cols = slice(KP * half, KP * (half + 1))
            nc.scalar.copy(out=g[:].bitcast(F32).rearrange("p (m u) -> p m u", u=2), in_=words[:, cols, :])
            page_g[b, half] = g

        def quantize_page(b, half):
            g = page_g[b, half]
            cols = slice(KP * half, KP * (half + 1))
            quantize(page_c[b, half], page_s[b][:, cols], g[:])

        first_product(0)
        features_on_vector(0)
        for s in range(1, PACK):
            first_product(s)
            features_on_scalar(s)
        features_on_gpsimd(1)
        for s in range(SLICES):
            scatter(s)
            if s == 0:
                for a in range(PASSES):
                    weave_w1(a, 1)
                pairs[0] = shared("w1_raw11", [P, 2, T2, 2], BF16, "pairs0")
            if s in (1, 2):
                quantize_w1(s - 1, 1)
            if s == 2:
                for later in range(PACK, SLICES):
                    first_product(later)
                    features_on_scalar(later)
            if s == PACK:
                weave_x0(0, 0)
                weave_page(0, 0)
                weave_page(0, 1)
            if s == 6:
                late = shared(H_SLOT[s], [P, 3, KP], U32, "late_codes")
                x0_c[0], page_c[0, 0], page_c[0, 1] = late[:, 0, :], late[:, 1, :], late[:, 2, :]
                quantize(x0_c[0], x0_s[0][:], x0_g[0][:])
                quantize_page(0, 0)
                quantize_page(0, 1)
            gather(s)
            round_page(s)
            if s + 2 < SLICES:
                features_on_gpsimd(s + 2)

        y_acc = [bank(s, "y_acc%d" % s) for s in range(SLICES)]

        def second_product(a):
            for s in range(SLICES):
                g = SLICES * a + s
                nc.tensor.matmul_mx(
                    out=y_acc[s][:], lhsT=w4_c[:, 2 * P * g : 2 * P * (g + 1)].bitcast(FP4X4),
                    lhsT_scale=w4_s[:, P * g : P * (g + 1)],
                    rhs=x0_c[a].bitcast(FP8X4), rhs_scale=x0_s[a][:],
                    start=(a == 0), stop=(a == PASSES - 1),
                )

        second_product(0)
        weave_x0(1, NP)
        last = kept([P, 3, KP], U32, "last_codes")
        x0_c[1], page_c[1, 0], page_c[1, 1] = last[:, 0, :], last[:, 1, :], last[:, 2, :]
        quantize(x0_c[1], x0_s[1][:], x0_g[1][:])
        second_product(1)
        x_c = [kept([P, NP], U32, "x_c%d" % b) for b in range(PASSES)]
        x_s = [kept([P, NP], U8, "x_s%d" % b) for b in range(PASSES)]
        x_pairs = [shared("x_pairs%d" % b, [P, 2, NP, 2], BF16, "x_pairs%d" % b) for b in range(PASSES)]
        x_g = {}

        def make_x(s):
            b, t = divmod(s, PACK)
            nc.vector.tensor_tensor(x0[b][:, t, :], y_acc[s][:], x0[b][:, t, :], ALU.min)
            nc.scalar.activation(
                out=x_pairs[b][:, t // 2, :, t % 2], in_=x0[b][:, t, :], func=ACT.Copy, scale=gain_sb[:, b, t : t + 1]
            )

        def weave_x(b):
            x_g[b] = grouped("x_g%d" % b)
            words = x_pairs[b][:].rearrange("p u m e -> p (u m e)").bitcast(F32).rearrange("p (u m) -> p m u", u=2)
            nc.vector.tensor_copy(out=x_g[b][:].bitcast(F32).rearrange("p (m u) -> p m u", u=2), in_=words)

        def third_product(b, i):
            cols = slice(P * i, P * (i + 1))
            nc.tensor.matmul_mx(
                out=e_acc[i][:],
                lhsT=page_c[b, i // PACK][:, P * (i % PACK) : P * (i % PACK + 1)].bitcast(FP8X4),
                lhsT_scale=page_s[b][:, cols],
                rhs=x_c[b][:].bitcast(FP8X4), rhs_scale=x_s[b][:],
                start=(b == 0), stop=(b == PASSES - 1),
            )

        weave_page(1, 0)
        weave_page(1, 1)
        for s in range(5):
            make_x(s)
        weave_x(0)
        make_x(5)
        quantize(x_c[0][:], x_s[0][:], x_g[0][:])
        make_x(6)
        quantize_page(1, 0)
        make_x(7)
        quantize_page(1, 1)
        weave_x(1)
        quantize(x_c[1][:], x_s[1][:], x_g[1][:])
        e_acc = [bank(i, "e_acc%d" % i) for i in range(SLICES)]
        for b in range(PASSES):
            for i in range(SLICES):
                third_product(b, i)
        scored = [shared(tag, [P, PACK, NP], F32, "scored_" + tag) for tag in ("x0_1", "x_pairs1")]
        for i in range(SLICES):
            nc.scalar.activation(
                out=scored[i // PACK][:, i % PACK, :], in_=base_sb[i // PACK][:, i % PACK, :],
                func=ACT.Copy, scale=slot_sb[:, i : i + 1],
            )
        for i in range(SLICES):
            res = scored[i // PACK][:, i % PACK, :]
            nc.vector.scalar_tensor_tensor(
                out=res, in0=e_acc[i][:], scalar=slot_sb[:, i : i + 1], in1=res, op0=ALU.mult, op1=ALU.subtract
            )
            nc.sync.dma_start(out=out[P * i : P * (i + 1), :], in_=res)
